import numpy as np
import ml_dtypes


def mxq(x, axis, fmt="e4m3"):
    dtype, down = {"e4m3": (ml_dtypes.float8_e4m3fn, 7), "e5m2": (ml_dtypes.float8_e5m2, 14)}[fmt]
    v = np.moveaxis(np.asarray(x, np.float32).astype(ml_dtypes.bfloat16).astype(np.float64), axis, -1)
    blocks = v.reshape(v.shape[:-1] + (-1, 32))
    amax = np.abs(blocks).max(-1, keepdims=True)
    byte = np.maximum(np.where(amax > 0, np.frexp(amax)[1] - 1 + 127, 0) - down, 1)
    scale = np.exp2(byte - 127.0)
    codes = (blocks / scale).astype(np.float32).astype(dtype).astype(np.float64)
    return np.moveaxis((codes * scale).reshape(v.shape), -1, axis)


WIDE = False


def mx_kscale(k):
    if not WIDE:
        return np.ones(k)
    levels = np.array([10, -10, 5, -5, 0])
    if k % 512:
        return np.exp2(np.random.permutation(np.resize(levels, k // 32))).repeat(32)
    a = np.empty((k // 512, 16))
    for p in range(k // 512):
        a[p, :8] = np.random.permutation(np.resize(levels, 8))
        for g in range(8):
            far = levels[np.abs(levels - a[p, g]) >= 10]
            a[p, g + 8] = far[np.random.randint(len(far))]
    return np.exp2(a.ravel()).repeat(32)


def f64(x):
    return np.asarray(x).astype(np.float64)


def striped(idx):
    return np.tile(idx.reshape(-1, 16).T, (8, 1)).astype(np.uint16)


def unstriped(offs):
    return offs[:16].T.reshape(-1).astype(np.int64)


E2M1 = np.array([0.0, 0.5, 1.0, 1.5, 2.0, 3.0, 4.0, 6.0, -0.0, -0.5, -1.0, -1.5, -2.0, -3.0, -4.0, -6.0])


def pack_weight(w, fmt):
    k, n = w.shape
    w = f64(np.asarray(w, np.float32).astype(ml_dtypes.bfloat16)).reshape(k // 32, 32, n)
    amax = np.abs(w).max(1)
    if fmt == "e4m3":
        byte = np.frexp(amax)[1] - 1 + 127 - 7
    else:
        mant, ex = np.frexp(amax / 6.0)
        byte = np.where(mant > 0.5, ex, ex - 1) + 127
    byte = np.clip(np.where(amax > 0, byte, 1), 1, 254)
    scaled = (w * np.exp2(127.0 - byte)[:, None, :]).reshape(k, n).astype(np.float32)
    by_word = np.ascontiguousarray(scaled.reshape(k // 512, 128, 4, n).transpose(0, 1, 3, 2))
    if fmt == "e4m3":
        words = by_word.astype(ml_dtypes.float8_e4m3fn).view(np.uint8)
    else:
        c = by_word.astype(ml_dtypes.float4_e2m1fn).view(np.uint8) & 0xF
        words = (c[..., 0::2] | (c[..., 1::2] << 4)).reshape(k // 512, 128, 2 * n)
    return np.ascontiguousarray(words), np.ascontiguousarray(byte.astype(np.uint8).reshape(k // 512, 16, n))


def unpack_weight(words, scales, fmt):
    g, _, n = scales.shape
    words = np.ascontiguousarray(words).reshape(g, 128, n, -1)
    if fmt == "e4m3":
        vals = words.view(ml_dtypes.float8_e4m3fn).astype(np.float64)
    else:
        nib = np.empty((g, 128, n, 4), np.uint8)
        nib[..., 0::2] = words & 0xF
        nib[..., 1::2] = words >> 4
        vals = E2M1[nib]
    vals = vals * np.repeat(np.exp2(scales.astype(np.float64) - 127.0), 8, axis=1)[..., None]
    return vals.transpose(0, 1, 3, 2).reshape(g * 512, n)


def gelu(v):
    return 0.5 * v * (1.0 + np.tanh(np.sqrt(2.0 / np.pi) * (v + 0.044715 * v**3)))


K, H, T, S, T2, P = 1536, 512, 4096, 1024, 2048, 1024

def setup_inputs():
    n = np.random.standard_normal
    s = mx_kscale(K)[:, None]
    u = mx_kscale(H)[:, None]
    d = {}
    d["tab_words"], d["tab_scales"] = pack_weight(n((K, T)) * s, "e4m3")
    d["offs"] = striped(np.random.permutation(T)[:S])
    d["w1"] = (n((K, H)) / s * u.T / K ** 0.5).astype(np.float32)
    d["page0"] = (n((H, T2)) * u).astype(np.float32)
    d["wgs"] = np.exp(0.3 * n((128, S))).astype(np.float32)
    d["offs2"] = striped(np.random.permutation(T2)[:S])
    d["offs3"] = striped(np.random.permutation(T2)[:P])
    d["offs4"] = striped(np.random.permutation(T2)[:P])
    d["sc"] = np.exp(0.4 * n(H)).astype(np.float32)
    d["w4_words"], d["w4_scales"] = pack_weight(1.2 * n((H, H)) / u / H ** 0.5, "e2m1")
    d["w3"] = (0.6 * n((H, H)) / u / H ** 0.5).astype(np.float32)
    d["ev"] = (1.2 * np.exp(0.3 * n(H)) / u[:, 0]).astype(np.float32)
    return d

def reference(tab_words, tab_scales, offs, w1, page0, wgs, offs2, offs3, offs4, sc, w4_words, w4_scales, w3, ev):
    v = unpack_weight(tab_words, tab_scales, "e4m3")[:, unstriped(offs)]
    h = mxq(f64(w1), 0, "e4m3").T @ v
    page = f64(page0).copy()
    page[:, unstriped(offs2)] = np.tile(f64(wgs), (H // 128, 1)) * h
    x = f64(sc)[:, None] * page[:, unstriped(offs3)]
    xq = mxq(x, 0, "e4m3")
    w4 = unpack_weight(w4_words, w4_scales, "e2m1")
    first = np.tanh(w4.T @ xq)
    second = mxq(f64(w3), 0, "e4m3").T @ xq
    y = second + first
    earlier = f64(ev)[:, None] * page[:, unstriped(offs4)]
    return y / (1.0 + np.abs(earlier))

@@ -1,0 +1,316 @@
+from contextlib import ExitStack
+
+import concourse.mybir as mybir
+from concourse.masks import make_identity
+
+K, H, T, S, T2, P = 1536, 512, 4096, 1024, 2048, 1024
+FLOPS = 2 * K * H * S + 2 * 2 * H * H * P
+
+F32 = mybir.dt.float32
+BF16 = mybir.dt.bfloat16
+I32 = mybir.dt.int32
+U32 = mybir.dt.uint32
+U16 = mybir.dt.uint16
+U8 = mybir.dt.uint8
+FP8X4 = mybir.dt.float8_e4m3fn_x4
+FP4X4 = mybir.dt.float4_e2m1fn_x4
+ACT = mybir.ActivationFunctionType
+ALU = mybir.AluOpType
+
+PARTS = 128
+PACK = 4
+K_PASS = PARTS * PACK
+PASSES = K // K_PASS
+BLOCKS = H // PARTS
+HALF = 512
+HALF_COLS = HALF // 16
+
+
+def interleave(nc, dst, src):
+    nc.scalar.copy(
+        out=dst.rearrange("p (c i) t -> p c t i", i=4),
+        in_=src.rearrange("p t (c i) -> p c t i", i=4),
+    )
+
+
+def tile_list_log_bay_scores_kernel(
+    tc, tab_words, tab_scales, offs, w1, page0, wgs, offs2, offs3, offs4, sc, w4_words, w4_scales, w3, ev, out
+):
+    nc = tc.nc
+    with ExitStack() as ctx:
+        keep = ctx.enter_context(tc.tile_pool(name="keep", bufs=1))
+        ring = ctx.enter_context(tc.tile_pool(name="ring", bufs=2))
+        psum = ctx.enter_context(tc.psum_pool(name="psum", bufs=8))
+
+        def bank(dtype=F32):
+            return psum.tile([PARTS, HALF], dtype, name="bank", tag="bank")
+
+        lists = [keep.tile([PARTS, S // 16], U16, name=f"list{i}") for i in range(4)]
+        idx, idx2, idx3, idx4 = lists
+
+        words = [keep.tile([PARTS, T], I32, name=f"words{a}", tag=f"big{a}") for a in range(PASSES)]
+        scales = keep.tile([PARTS, T], U8, name="scales")
+        w4s = keep.tile([PARTS, H], U8, name="w4s", align_bytes=64)
+        w4w = keep.tile([PARTS, 2 * H], U8, name="w4w", align_bytes=64)
+        w1_first = [keep.tile([PARTS, PACK, PARTS], F32, name=f"w1_first{a}") for a in range(PASSES)]
+        w1_rest = [keep.tile([PARTS, PACK, H - PARTS], F32, name=f"w1_rest{a}") for a in range(PASSES)]
+        page = [keep.tile([PARTS, T2], F32, name=f"page{m}") for m in range(BLOCKS)]
+        gains = keep.tile([PARTS, S], F32, name="gains")
+        w3_raw = keep.tile([PARTS, PACK, H], F32, name="w3_raw")
+        sc_col = keep.tile([PARTS, BLOCKS], F32, name="sc_col")
+        ev_col = keep.tile([PARTS, BLOCKS], F32, name="ev_col")
+        ident_bf = keep.tile([PARTS, PARTS], BF16, name="ident_bf")
+        ident_f32 = keep.tile([PARTS, PARTS], F32, name="ident_f32")
+
+        def w1_rows(a):
+            return w1[a * K_PASS : (a + 1) * K_PASS, :].rearrange("(p i) c -> p i c", i=PACK)
+
+        def load_words(a):
+            nc.sync.dma_start(out=words[a][:], in_=tab_words[a].rearrange("p t i -> p (t i)").bitcast(I32))
+
+        def load_page(m):
+            nc.sync.dma_start(out=page[m][:], in_=page0[m * PARTS : (m + 1) * PARTS, :])
+
+        nc.vector.memset(scales[:].bitcast(I32), 0)
+        nc.vector.memset(w4s[:].bitcast(I32), 0)
+        for q in range(4):
+            nc.scalar.dma_start(
+                out=scales[32 * q : 32 * q + 4 * PASSES, :].bitcast(I32),
+                in_=tab_scales[:, 4 * q : 4 * q + 4, :].bitcast(I32),
+            )
+        make_identity(nc, ident_bf[:])
+        make_identity(nc, ident_f32[:])
+
+        nc.sync.dma_start(idx[:], offs)
+        load_words(0)
+        for a in range(PASSES):
+            nc.sync.dma_start(out=w1_first[a][:], in_=w1_rows(a)[:, :, 0:PARTS])
+        load_words(1)
+        load_words(2)
+        load_page(0)
+        nc.sync.dma_start(idx2[:], offs2)
+        nc.sync.dma_start(out=gains[:, 0:HALF], in_=wgs[:, 0:HALF])
+        nc.sync.dma_start(out=gains[:, HALF:S], in_=wgs[:, HALF:S])
+        for a in range(PASSES):
+            nc.sync.dma_start(out=w1_rest[a][:], in_=w1_rows(a)[:, :, PARTS:H])
+        nc.sync.dma_start(idx3[:], offs3)
+        nc.sync.dma_start(idx4[:], offs4)
+        load_page(1)
+        with nc.allow_non_contiguous_dma(reason="one value a partition"):
+            nc.sync.dma_start(out=sc_col[:], in_=sc.rearrange("(m p) -> p m", p=PARTS))
+            nc.sync.dma_start(out=ev_col[:], in_=ev.rearrange("(m p) -> p m", p=PARTS))
+        load_page(2)
+        load_page(3)
+        nc.sync.dma_start(out=w3_raw[:], in_=w3.rearrange("(p i) c -> p i c", i=PACK))
+        nc.sync.dma_start(out=w4w[:].bitcast(I32), in_=w4_words[0].bitcast(I32))
+        for q in range(4):
+            nc.sync.dma_start(
+                out=w4s[32 * q : 32 * q + 4, :].bitcast(I32), in_=w4_scales[0, 4 * q : 4 * q + 4, :].bitcast(I32)
+            )
+
+        picked_words = [keep.tile([PARTS, S], U32, name=f"picked{a}", align_bytes=64) for a in range(PASSES)]
+        picked_scales = keep.tile([PARTS, S], U8, name="picked_scales", align_bytes=64)
+        w1_codes = [keep.tile([PARTS, PASSES * PARTS], U32, name=f"w1_codes{m}", align_bytes=64) for m in range(BLOCKS)]
+        w1_scales = [keep.tile([PARTS, PASSES * PARTS], U8, name=f"w1_scales{m}", align_bytes=64) for m in range(BLOCKS)]
+        h = [keep.tile([PARTS, S], F32, name=f"h{m}") for m in range(BLOCKS)]
+
+        def quantise_w1(m):
+            two = keep.tile([PARTS, 2, PARTS, PACK], BF16, name=f"w1_two{m}", tag=f"shared_a{m}", align_bytes=64)
+            one = keep.tile([PARTS, 1, PARTS, PACK], BF16, name=f"w1_one{m}", tag=f"shared_b{m}", align_bytes=64)
+            for a in range(PASSES):
+                src = w1_first[a][:] if m == 0 else w1_rest[a][:, :, (m - 1) * PARTS : m * PARTS]
+                interleave(nc, two[:, a] if a < 2 else one[:, 0], src)
+            nc.vector.quantize_mx(
+                out=w1_codes[m][:, 0 : 2 * PARTS].bitcast(FP8X4),
+                scales=w1_scales[m][:, 0 : 2 * PARTS],
+                in_=two[:].rearrange("p a c t -> p (a c t)"),
+            )
+            nc.vector.quantize_mx(
+                out=w1_codes[m][:, 2 * PARTS : 3 * PARTS].bitcast(FP8X4),
+                scales=w1_scales[m][:, 2 * PARTS : 3 * PARTS],
+                in_=one[:].rearrange("p a c t -> p (a c t)"),
+            )
+
+        def make_h(m, half):
+            cols = slice(half * HALF, (half + 1) * HALF)
+            acc = bank()
+            for a in range(PASSES):
+                nc.tensor.matmul_mx(
+                    out=acc[:],
+                    lhsT=w1_codes[m][:, a * PARTS : (a + 1) * PARTS].bitcast(FP8X4),
+                    lhsT_scale=w1_scales[m][:, a * PARTS : (a + 1) * PARTS],
+                    rhs=picked_words[a][:, cols].bitcast(FP8X4),
+                    rhs_scale=picked_scales[4 * a : PARTS, cols],
+                    start=(a == 0),
+                    stop=(a == PASSES - 1),
+                )
+            nc.scalar.copy(out=h[m][:, cols], in_=acc[:])
+
+        nc.vector.tensor_copy(picked_words[0][:], words[0][:].bitcast(U32).indirect(idx[:]))
+        nc.vector.tensor_copy(picked_scales[:], scales[:].indirect(idx[:]))
+        quantise_w1(0)
+        nc.vector.tensor_copy(picked_words[1][:], words[1][:].bitcast(U32).indirect(idx[:]))
+        for half in range(2):
+            nc.vector.tensor_copy(
+                picked_words[2][:, half * HALF : (half + 1) * HALF],
+                words[2][:].bitcast(U32).indirect(idx[:, half * HALF_COLS : (half + 1) * HALF_COLS]),
+            )
+        for half in range(2):
+            make_h(0, half)
+        for half in range(2):
+            cols = slice(half * HALF, (half + 1) * HALF)
+            nc.vector.tensor_tensor(
+                page[0][:].indirect(idx2[:, half * HALF_COLS : (half + 1) * HALF_COLS]),
+                h[0][:, cols],
+                gains[:, cols],
+                ALU.mult,
+            )
+        for m in range(1, BLOCKS):
+            quantise_w1(m)
+            for half in range(2):
+                make_h(m, half)
+
+        chunks = [slice(0, 256), slice(256, 512), slice(512, 1024)]
+        widths = [c.stop - c.start for c in chunks]
+        x_turned = [keep.tile([PARTS, n // PARTS, 2, PARTS], F32, name=f"x_turned{c}") for c, n in enumerate(widths)]
+        damp = keep.tile([PARTS, BLOCKS, P], F32, name="damp", tag="big0")
+        scratch = keep.tile([PARTS, 2 * BLOCKS * HALF], F32, name="scratch", tag="big1")
+        scores = keep.tile([PARTS, BLOCKS, P], F32, name="scores", tag="big2")
+        w3_codes = keep.tile([PARTS, H], U32, name="w3_codes", align_bytes=64)
+        w3_scales = keep.tile([PARTS, H], U8, name="w3_scales", align_bytes=64)
+
+        def turn_x(m, which, ready):
+            n = sum(widths[c] for c in which)
+            x_rows = keep.tile([PARTS, n], BF16, name="x_rows", tag="x_rows")
+            nc.scalar.activation(x_rows[:], ready, ACT.Copy, scale=sc_col[:, m : m + 1])
+            turned = bank(BF16)
+            for jb in range(n // PARTS):
+                nc.tensor.transpose(turned[:, jb * PARTS : (jb + 1) * PARTS], x_rows[:, jb * PARTS : (jb + 1) * PARTS], ident_bf[:])
+            at = 0
+            for c in which:
+                nc.scalar.copy(
+                    out=x_turned[c][:, :, :, 32 * m : 32 * m + 32],
+                    in_=turned[:, at : at + widths[c]].bitcast(F32).rearrange("p (b q u) -> p b u q", q=32, u=2),
+                )
+                at = at + widths[c]
+
+        def make_damp(m, cols, earlier, mag, root):
+            nc.scalar.activation(mag, earlier, ACT.Abs, scale=ev_col[:, m : m + 1])
+            nc.scalar.activation(root, mag, ACT.Abs_reciprocal_sqrt, bias=1.0)
+            nc.scalar.activation(damp[:, m, cols], root, ACT.Square)
+
+        x_codes = [keep.tile([PARTS, n], U32, name=f"x_codes{c}", align_bytes=64) for c, n in enumerate(widths)]
+        x_scales = [keep.tile([PARTS, n], U8, name=f"x_scales{c}", align_bytes=64) for c, n in enumerate(widths)]
+
+        def quantise_x(c):
+            grouped = keep.tile([PARTS, widths[c] * PACK], BF16, name=f"x_grouped{c}", tag=f"x_grouped{c}", align_bytes=64)
+            for pair in range(widths[c] // 256):
+                back = bank()
+                for b in range(2):
+                    for u in range(2):
+                        nc.tensor.transpose(
+                            back[:, (2 * b + u) * PARTS : (2 * b + u + 1) * PARTS],
+                            x_turned[c][:, 2 * pair + b, u, :],
+                            ident_f32[:],
+                        )
+                nc.scalar.copy(
+                    out=grouped[:].bitcast(F32)[:, pair * HALF : (pair + 1) * HALF].rearrange("p (b j u) -> p b j u", b=2, u=2),
+                    in_=back[:].rearrange("p (b u j) -> p b j u", b=2, u=2),
+                )
+            nc.vector.quantize_mx(out=x_codes[c][:].bitcast(FP8X4), scales=x_scales[c][:], in_=grouped[:])
+
+        def pick(dst, m, lst, cols):
+            nc.vector.tensor_copy(dst, page[m][:].indirect(lst[:, cols.start // 16 : cols.stop // 16]))
+
+        for m in range(BLOCKS - 1):
+            if m > 0:
+                nc.vector.tensor_tensor(page[m][:].indirect(idx2[:]), h[m][:], gains[:], ALU.mult)
+            ready = keep.tile([PARTS, P], F32, name=f"ready{m}", tag=f"shared_a{m + 1}", align_bytes=64)
+            earlier = keep.tile([PARTS, P], F32, name=f"earlier{m}", tag=f"shared_b{m + 1}", align_bytes=64)
+            pick(ready[:], m, idx3, slice(0, P))
+            pick(earlier[:], m, idx4, slice(0, P))
+            turn_x(m, [0, 1], ready[:, 0:HALF])
+            turn_x(m, [2], ready[:, HALF:P])
+            first_col = (m % 2) * 2 * P
+            make_damp(m, slice(0, P), earlier[:], scratch[:, first_col : first_col + P], scratch[:, first_col + P : first_col + 2 * P])
+            if m == BLOCKS - 2:
+                warm = keep.tile([PARTS, 1], F32, name="warm")
+                nc.scalar.activation(warm[:], scratch[:, first_col + P : first_col + P + 1], ACT.Tanh)
+            if m == 0:
+                w3_grouped = keep.tile([PARTS, H, PACK], BF16, name="w3_grouped", align_bytes=64)
+                interleave(nc, w3_grouped[:], w3_raw[:])
+                nc.vector.quantize_mx(
+                    out=w3_codes[:].bitcast(FP8X4), scales=w3_scales[:], in_=w3_grouped[:].rearrange("p c t -> p (c t)")
+                )
+
+        def score(c, blocks, unit):
+            n = widths[c]
+            first = bank()
+            second = bank()
+            for i, m in enumerate(blocks):
+                nc.tensor.matmul_mx(
+                    out=first[:, i * n : (i + 1) * n],
+                    lhsT=w4w[:, 2 * m * PARTS : 2 * (m + 1) * PARTS].bitcast(FP4X4),
+                    lhsT_scale=w4s[:, m * PARTS : (m + 1) * PARTS],
+                    rhs=x_codes[c][:].bitcast(FP8X4),
+                    rhs_scale=x_scales[c][:],
+                    start=True,
+                    stop=True,
+                )
+            for i, m in enumerate(blocks):
+                nc.tensor.matmul_mx(
+                    out=second[:, i * n : (i + 1) * n],
+                    lhsT=w3_codes[:, m * PARTS : (m + 1) * PARTS].bitcast(FP8X4),
+                    lhsT_scale=w3_scales[:, m * PARTS : (m + 1) * PARTS],
+                    rhs=x_codes[c][:].bitcast(FP8X4),
+                    rhs_scale=x_scales[c][:],
+                    start=True,
+                    stop=True,
+                )
+            bounded = scratch[:, unit * HALF : (unit + 1) * HALF]
+            nc.scalar.activation(bounded, first[:], ACT.Tanh)
+            nc.vector.tensor_tensor(
+                scores[:, blocks[0] : blocks[-1] + 1, chunks[c]],
+                second[:].rearrange("p (b j) -> p b j", j=n),
+                bounded.rearrange("p (b j) -> p b j", j=n),
+                ALU.add,
+            )
+
+        def finish(m, half):
+            cols = slice(half * HALF, (half + 1) * HALF)
+            nc.vector.tensor_tensor(scores[:, m, cols], scores[:, m, cols], damp[:, m, cols], ALU.mult)
+            nc.sync.dma_start(out=out[m * PARTS : (m + 1) * PARTS, cols], in_=scores[:, m, cols])
+
+        m = BLOCKS - 1
+        nc.vector.tensor_tensor(page[m][:].indirect(idx2[:]), h[m][:], gains[:], ALU.mult)
+        ready = keep.tile([PARTS, P], F32, name="ready_last")
+        for c in range(3):
+            pick(ready[:, chunks[c]], m, idx3, chunks[c])
+        earlier_a = keep.tile([PARTS, HALF], F32, name="earlier_a")
+        pick(earlier_a[:], m, idx4, slice(0, HALF))
+        turn_x(m, [0], ready[:, chunks[0]])
+        quantise_x(0)
+        earlier_b = keep.tile([PARTS, HALF], F32, name="earlier_b", tag="x_grouped0", align_bytes=64)
+        pick(earlier_b[:], m, idx4, slice(HALF, P))
+        turn_x(m, [1], ready[:, chunks[1]])
+        quantise_x(1)
+        turn_x(m, [2], ready[:, chunks[2]])
+        score(0, [0, 1], 0)
+        quantise_x(2)
+        score(0, [2, 3], 1)
+        score(1, [0, 1], 2)
+        finish(0, 0)
+        finish(1, 0)
+        score(1, [2, 3], 3)
+        finish(2, 0)
+        for i in range(BLOCKS):
+            score(2, [i], BLOCKS + i)
+            if i < BLOCKS - 1:
+                finish(i, 1)
+        for half, earlier in enumerate((earlier_a, earlier_b)):
+            cols = slice(half * HALF, (half + 1) * HALF)
+            mag = keep.tile([PARTS, HALF], F32, name=f"mag{half}", tag="x_rows" if half == 0 else "mag")
+            root = scratch[:, (BLOCKS + half) * HALF : (BLOCKS + half + 1) * HALF]
+            make_damp(m, cols, earlier[:], mag[:], root)
+        for half in range(2):
+            finish(m, half)

@@ -49,7 +49,7 @@ def tile_list_log_bay_scores_kernel(
         idx, idx2, idx3, idx4 = lists
 
         words = [keep.tile([PARTS, T], I32, name=f"words{a}", tag=f"big{a}") for a in range(PASSES)]
-        scales = keep.tile([PARTS, T], U8, name="scales")
+        scales = keep.tile([PARTS, T], U8, name="scales", tag="picked1", align_bytes=64)
         w4s = keep.tile([PARTS, H], U8, name="w4s", align_bytes=64)
         w4w = keep.tile([PARTS, 2 * H], U8, name="w4w", align_bytes=64)
         w1_first = [keep.tile([PARTS, PACK, PARTS], F32, name=f"w1_first{a}") for a in range(PASSES)]
@@ -74,7 +74,7 @@ def tile_list_log_bay_scores_kernel(
         nc.vector.memset(scales[:].bitcast(I32), 0)
         nc.vector.memset(w4s[:].bitcast(I32), 0)
         for q in range(4):
-            nc.scalar.dma_start(
+            nc.gpsimd.dma_start(
                 out=scales[32 * q : 32 * q + 4 * PASSES, :].bitcast(I32),
                 in_=tab_scales[:, 4 * q : 4 * q + 4, :].bitcast(I32),
             )
@@ -108,7 +108,7 @@ def tile_list_log_bay_scores_kernel(
                 out=w4s[32 * q : 32 * q + 4, :].bitcast(I32), in_=w4_scales[0, 4 * q : 4 * q + 4, :].bitcast(I32)
             )
 
-        picked_words = [keep.tile([PARTS, S], U32, name=f"picked{a}", align_bytes=64) for a in range(PASSES)]
+        picked_words = [keep.tile([PARTS, S], U32, name=f"picked{a}", tag=f"picked{a}", align_bytes=64) for a in range(PASSES)]
         picked_scales = keep.tile([PARTS, S], U8, name="picked_scales", align_bytes=64)
         w1_codes = [keep.tile([PARTS, PASSES * PARTS], U32, name=f"w1_codes{m}", align_bytes=64) for m in range(BLOCKS)]
         w1_scales = [keep.tile([PARTS, PASSES * PARTS], U8, name=f"w1_scales{m}", align_bytes=64) for m in range(BLOCKS)]
@@ -172,16 +172,16 @@ def tile_list_log_bay_scores_kernel(
 
         chunks = [slice(0, 256), slice(256, 512), slice(512, 1024)]
         widths = [c.stop - c.start for c in chunks]
-        x_turned = [keep.tile([PARTS, n // PARTS, 2, PARTS], F32, name=f"x_turned{c}") for c, n in enumerate(widths)]
+        x_turned = [keep.tile([PARTS, n // PARTS, 2, PARTS], F32, name=f"x_turned{c}", tag=f"x_turned{c}") for c, n in enumerate(widths)]
         damp = keep.tile([PARTS, BLOCKS, P], F32, name="damp", tag="big0")
         scratch = keep.tile([PARTS, 2 * BLOCKS * HALF], F32, name="scratch", tag="big1")
         scores = keep.tile([PARTS, BLOCKS, P], F32, name="scores", tag="big2")
         w3_codes = keep.tile([PARTS, H], U32, name="w3_codes", align_bytes=64)
         w3_scales = keep.tile([PARTS, H], U8, name="w3_scales", align_bytes=64)
 
-        def turn_x(m, which, ready):
+        def turn_x(m, which, ready, tag):
             n = sum(widths[c] for c in which)
-            x_rows = keep.tile([PARTS, n], BF16, name="x_rows", tag="x_rows")
+            x_rows = keep.tile([PARTS, n], BF16, name="x_rows", tag=tag)
             nc.scalar.activation(x_rows[:], ready, ACT.Copy, scale=sc_col[:, m : m + 1])
             turned = bank(BF16)
             for jb in range(n // PARTS):
@@ -229,8 +229,8 @@ def tile_list_log_bay_scores_kernel(
             earlier = keep.tile([PARTS, P], F32, name=f"earlier{m}", tag=f"shared_b{m + 1}", align_bytes=64)
             pick(ready[:], m, idx3, slice(0, P))
             pick(earlier[:], m, idx4, slice(0, P))
-            turn_x(m, [0, 1], ready[:, 0:HALF])
-            turn_x(m, [2], ready[:, HALF:P])
+            turn_x(m, [0, 1], ready[:, 0:HALF], "x_rows0")
+            turn_x(m, [2], ready[:, HALF:P], "x_rows0")
             first_col = (m % 2) * 2 * P
             make_damp(m, slice(0, P), earlier[:], scratch[:, first_col : first_col + P], scratch[:, first_col + P : first_col + 2 * P])
             if m == BLOCKS - 2:
@@ -286,31 +286,34 @@ def tile_list_log_bay_scores_kernel(
         ready = keep.tile([PARTS, P], F32, name="ready_last")
         for c in range(3):
             pick(ready[:, chunks[c]], m, idx3, chunks[c])
-        earlier_a = keep.tile([PARTS, HALF], F32, name="earlier_a")
-        pick(earlier_a[:], m, idx4, slice(0, HALF))
-        turn_x(m, [0], ready[:, chunks[0]])
+        pieces = [slice(0, 768), slice(768, 1024)]
+        earlier_a = keep.tile([PARTS, 768], F32, name="earlier_a")
+        pick(earlier_a[:], m, idx4, pieces[0])
+        turn_x(m, [0], ready[:, chunks[0]], "x_rows0")
+        turn_x(m, [1], ready[:, chunks[1]], "x_rows1")
         quantise_x(0)
-        earlier_b = keep.tile([PARTS, HALF], F32, name="earlier_b", tag="x_grouped0", align_bytes=64)
-        pick(earlier_b[:], m, idx4, slice(HALF, P))
-        turn_x(m, [1], ready[:, chunks[1]])
+        earlier_b = keep.tile([PARTS, 256], F32, name="earlier_b", tag="x_grouped0", align_bytes=64)
+        pick(earlier_b[:], m, idx4, pieces[1])
+        turn_x(m, [2], ready[:, chunks[2]], "x_rows1")
         quantise_x(1)
-        turn_x(m, [2], ready[:, chunks[2]])
-        score(0, [0, 1], 0)
         quantise_x(2)
+        score(0, [0, 1], 0)
         score(0, [2, 3], 1)
         score(1, [0, 1], 2)
-        finish(0, 0)
-        finish(1, 0)
         score(1, [2, 3], 3)
-        finish(2, 0)
         for i in range(BLOCKS):
-            score(2, [i], BLOCKS + i)
             if i < BLOCKS - 1:
-                finish(i, 1)
-        for half, earlier in enumerate((earlier_a, earlier_b)):
+                finish(i, 0)
+            score(2, [i], BLOCKS + i)
+        for i in range(BLOCKS - 1):
+            finish(i, 1)
+        mag = keep.tile([PARTS, P], F32, name="mag", tag="x_grouped1", align_bytes=64)
+        for cols, piece in zip(pieces, (earlier_a, earlier_b)):
+            nc.scalar.activation(mag[:, cols], piece[:], ACT.Abs, scale=ev_col[:, m : m + 1])
+        for half in range(2):
             cols = slice(half * HALF, (half + 1) * HALF)
-            mag = keep.tile([PARTS, HALF], F32, name=f"mag{half}", tag="x_rows" if half == 0 else "mag")
             root = scratch[:, (BLOCKS + half) * HALF : (BLOCKS + half + 1) * HALF]
-            make_damp(m, cols, earlier[:], mag[:], root)
+            nc.scalar.activation(root, mag[:, cols], ACT.Abs_reciprocal_sqrt, bias=1.0)
+            nc.scalar.activation(damp[:, m, cols], root, ACT.Square)
         for half in range(2):
             finish(m, half)

from contextlib import ExitStack

import concourse.mybir as mybir
from concourse.masks import make_identity

K, H, T, S, T2, P = 1536, 512, 4096, 1024, 2048, 1024
FLOPS = 2 * K * H * S + 2 * 2 * H * H * P

F32 = mybir.dt.float32
BF16 = mybir.dt.bfloat16
I32 = mybir.dt.int32
U32 = mybir.dt.uint32
U16 = mybir.dt.uint16
U8 = mybir.dt.uint8
FP8X4 = mybir.dt.float8_e4m3fn_x4
FP4X4 = mybir.dt.float4_e2m1fn_x4
ACT = mybir.ActivationFunctionType
ALU = mybir.AluOpType

PARTS = 128
PACK = 4
K_PASS = PARTS * PACK
PASSES = K // K_PASS
BLOCKS = H // PARTS
HALF = 512
HALF_COLS = HALF // 16


def interleave(nc, dst, src):
    nc.scalar.copy(
        out=dst.rearrange("p (c i) t -> p c t i", i=4),
        in_=src.rearrange("p t (c i) -> p c t i", i=4),
    )


def tile_list_log_bay_scores_kernel(
    tc, tab_words, tab_scales, offs, w1, page0, wgs, offs2, offs3, offs4, sc, w4_words, w4_scales, w3, ev, out
):
    nc = tc.nc
    with ExitStack() as ctx:
        keep = ctx.enter_context(tc.tile_pool(name="keep", bufs=1))
        ring = ctx.enter_context(tc.tile_pool(name="ring", bufs=2))
        psum = ctx.enter_context(tc.psum_pool(name="psum", bufs=8))

        def bank(dtype=F32):
            return psum.tile([PARTS, HALF], dtype, name="bank", tag="bank")

        lists = [keep.tile([PARTS, S // 16], U16, name=f"list{i}") for i in range(4)]
        idx, idx2, idx3, idx4 = lists

        words = [keep.tile([PARTS, T], I32, name=f"words{a}", tag=f"big{a}") for a in range(PASSES)]
        scales = keep.tile([PARTS, T], U8, name="scales", tag="picked1", align_bytes=64)
        w4s = keep.tile([PARTS, H], U8, name="w4s", align_bytes=64)
        w4w = keep.tile([PARTS, 2 * H], U8, name="w4w", align_bytes=64)
        w1_first = [keep.tile([PARTS, PACK, PARTS], F32, name=f"w1_first{a}") for a in range(PASSES)]
        w1_rest = [keep.tile([PARTS, PACK, H - PARTS], F32, name=f"w1_rest{a}") for a in range(PASSES)]
        page = [keep.tile([PARTS, T2], F32, name=f"page{m}") for m in range(BLOCKS)]
        gains = keep.tile([PARTS, S], F32, name="gains")
        w3_raw = keep.tile([PARTS, PACK, H], F32, name="w3_raw")
        sc_col = keep.tile([PARTS, BLOCKS], F32, name="sc_col")
        ev_col = keep.tile([PARTS, BLOCKS], F32, name="ev_col")
        ident_bf = keep.tile([PARTS, PARTS], BF16, name="ident_bf")
        ident_f32 = keep.tile([PARTS, PARTS], F32, name="ident_f32")

        def w1_rows(a):
            return w1[a * K_PASS : (a + 1) * K_PASS, :].rearrange("(p i) c -> p i c", i=PACK)

        def load_words(a):
            nc.sync.dma_start(out=words[a][:], in_=tab_words[a].rearrange("p t i -> p (t i)").bitcast(I32))

        def load_page(m):
            nc.sync.dma_start(out=page[m][:], in_=page0[m * PARTS : (m + 1) * PARTS, :])

        nc.vector.memset(scales[:].bitcast(I32), 0)
        nc.vector.memset(w4s[:].bitcast(I32), 0)
        for q in range(4):
            nc.gpsimd.dma_start(
                out=scales[32 * q : 32 * q + 4 * PASSES, :].bitcast(I32),
                in_=tab_scales[:, 4 * q : 4 * q + 4, :].bitcast(I32),
            )
        make_identity(nc, ident_bf[:])
        make_identity(nc, ident_f32[:])

        nc.sync.dma_start(idx[:], offs)
        load_words(0)
        for a in range(PASSES):
            nc.sync.dma_start(out=w1_first[a][:], in_=w1_rows(a)[:, :, 0:PARTS])
        load_words(1)
        load_words(2)
        load_page(0)
        nc.sync.dma_start(idx2[:], offs2)
        nc.sync.dma_start(out=gains[:, 0:HALF], in_=wgs[:, 0:HALF])
        nc.sync.dma_start(out=gains[:, HALF:S], in_=wgs[:, HALF:S])
        for a in range(PASSES):
            nc.sync.dma_start(out=w1_rest[a][:], in_=w1_rows(a)[:, :, PARTS:H])
        nc.sync.dma_start(idx3[:], offs3)
        nc.sync.dma_start(idx4[:], offs4)
        load_page(1)
        with nc.allow_non_contiguous_dma(reason="one value a partition"):
            nc.sync.dma_start(out=sc_col[:], in_=sc.rearrange("(m p) -> p m", p=PARTS))
            nc.sync.dma_start(out=ev_col[:], in_=ev.rearrange("(m p) -> p m", p=PARTS))
        load_page(2)
        load_page(3)
        nc.sync.dma_start(out=w3_raw[:], in_=w3.rearrange("(p i) c -> p i c", i=PACK))
        nc.sync.dma_start(out=w4w[:].bitcast(I32), in_=w4_words[0].bitcast(I32))
        for q in range(4):
            nc.sync.dma_start(
                out=w4s[32 * q : 32 * q + 4, :].bitcast(I32), in_=w4_scales[0, 4 * q : 4 * q + 4, :].bitcast(I32)
            )

        picked_words = [keep.tile([PARTS, S], U32, name=f"picked{a}", tag=f"picked{a}", align_bytes=64) for a in range(PASSES)]
        picked_scales = keep.tile([PARTS, S], U8, name="picked_scales", align_bytes=64)
        w1_codes = [keep.tile([PARTS, PASSES * PARTS], U32, name=f"w1_codes{m}", align_bytes=64) for m in range(BLOCKS)]
        w1_scales = [keep.tile([PARTS, PASSES * PARTS], U8, name=f"w1_scales{m}", align_bytes=64) for m in range(BLOCKS)]
        h = [keep.tile([PARTS, S], F32, name=f"h{m}") for m in range(BLOCKS)]

        def quantise_w1(m):
            two = keep.tile([PARTS, 2, PARTS, PACK], BF16, name=f"w1_two{m}", tag=f"shared_a{m}", align_bytes=64)
            one = keep.tile([PARTS, 1, PARTS, PACK], BF16, name=f"w1_one{m}", tag=f"shared_b{m}", align_bytes=64)
            for a in range(PASSES):
                src = w1_first[a][:] if m == 0 else w1_rest[a][:, :, (m - 1) * PARTS : m * PARTS]
                interleave(nc, two[:, a] if a < 2 else one[:, 0], src)
            nc.vector.quantize_mx(
                out=w1_codes[m][:, 0 : 2 * PARTS].bitcast(FP8X4),
                scales=w1_scales[m][:, 0 : 2 * PARTS],
                in_=two[:].rearrange("p a c t -> p (a c t)"),
            )
            nc.vector.quantize_mx(
                out=w1_codes[m][:, 2 * PARTS : 3 * PARTS].bitcast(FP8X4),
                scales=w1_scales[m][:, 2 * PARTS : 3 * PARTS],
                in_=one[:].rearrange("p a c t -> p (a c t)"),
            )

        def make_h(m, half):
            cols = slice(half * HALF, (half + 1) * HALF)
            acc = bank()
            for a in range(PASSES):
                nc.tensor.matmul_mx(
                    out=acc[:],
                    lhsT=w1_codes[m][:, a * PARTS : (a + 1) * PARTS].bitcast(FP8X4),
                    lhsT_scale=w1_scales[m][:, a * PARTS : (a + 1) * PARTS],
                    rhs=picked_words[a][:, cols].bitcast(FP8X4),
                    rhs_scale=picked_scales[4 * a : PARTS, cols],
                    start=(a == 0),
                    stop=(a == PASSES - 1),
                )
            nc.scalar.copy(out=h[m][:, cols], in_=acc[:])

        nc.vector.tensor_copy(picked_words[0][:], words[0][:].bitcast(U32).indirect(idx[:]))
        nc.vector.tensor_copy(picked_scales[:], scales[:].indirect(idx[:]))
        quantise_w1(0)
        nc.vector.tensor_copy(picked_words[1][:], words[1][:].bitcast(U32).indirect(idx[:]))
        for half in range(2):
            nc.vector.tensor_copy(
                picked_words[2][:, half * HALF : (half + 1) * HALF],
                words[2][:].bitcast(U32).indirect(idx[:, half * HALF_COLS : (half + 1) * HALF_COLS]),
            )
        for half in range(2):
            make_h(0, half)
        for half in range(2):
            cols = slice(half * HALF, (half + 1) * HALF)
            nc.vector.tensor_tensor(
                page[0][:].indirect(idx2[:, half * HALF_COLS : (half + 1) * HALF_COLS]),
                h[0][:, cols],
                gains[:, cols],
                ALU.mult,
            )
        for m in range(1, BLOCKS):
            quantise_w1(m)
            for half in range(2):
                make_h(m, half)

        chunks = [slice(0, 256), slice(256, 512), slice(512, 1024)]
        widths = [c.stop - c.start for c in chunks]
        x_turned = [keep.tile([PARTS, n // PARTS, 2, PARTS], F32, name=f"x_turned{c}", tag=f"x_turned{c}") for c, n in enumerate(widths)]
        damp = keep.tile([PARTS, BLOCKS, P], F32, name="damp", tag="big0")
        scratch = keep.tile([PARTS, 2 * BLOCKS * HALF], F32, name="scratch", tag="big1")
        scores = keep.tile([PARTS, BLOCKS, P], F32, name="scores", tag="big2")
        w3_codes = keep.tile([PARTS, H], U32, name="w3_codes", align_bytes=64)
        w3_scales = keep.tile([PARTS, H], U8, name="w3_scales", align_bytes=64)

        def turn_x(m, which, ready, tag):
            n = sum(widths[c] for c in which)
            x_rows = keep.tile([PARTS, n], BF16, name="x_rows", tag=tag)
            nc.scalar.activation(x_rows[:], ready, ACT.Copy, scale=sc_col[:, m : m + 1])
            turned = bank(BF16)
            for jb in range(n // PARTS):
                nc.tensor.transpose(turned[:, jb * PARTS : (jb + 1) * PARTS], x_rows[:, jb * PARTS : (jb + 1) * PARTS], ident_bf[:])
            at = 0
            for c in which:
                nc.scalar.copy(
                    out=x_turned[c][:, :, :, 32 * m : 32 * m + 32],
                    in_=turned[:, at : at + widths[c]].bitcast(F32).rearrange("p (b q u) -> p b u q", q=32, u=2),
                )
                at = at + widths[c]

        def make_damp(m, cols, earlier, mag, root):
            nc.scalar.activation(mag, earlier, ACT.Abs, scale=ev_col[:, m : m + 1])
            nc.scalar.activation(root, mag, ACT.Abs_reciprocal_sqrt, bias=1.0)
            nc.scalar.activation(damp[:, m, cols], root, ACT.Square)

        x_codes = [keep.tile([PARTS, n], U32, name=f"x_codes{c}", align_bytes=64) for c, n in enumerate(widths)]
        x_scales = [keep.tile([PARTS, n], U8, name=f"x_scales{c}", align_bytes=64) for c, n in enumerate(widths)]

        def quantise_x(c):
            grouped = keep.tile([PARTS, widths[c] * PACK], BF16, name=f"x_grouped{c}", tag=f"x_grouped{c}", align_bytes=64)
            for pair in range(widths[c] // 256):
                back = bank()
                for b in range(2):
                    for u in range(2):
                        nc.tensor.transpose(
                            back[:, (2 * b + u) * PARTS : (2 * b + u + 1) * PARTS],
                            x_turned[c][:, 2 * pair + b, u, :],
                            ident_f32[:],
                        )
                nc.scalar.copy(
                    out=grouped[:].bitcast(F32)[:, pair * HALF : (pair + 1) * HALF].rearrange("p (b j u) -> p b j u", b=2, u=2),
                    in_=back[:].rearrange("p (b u j) -> p b j u", b=2, u=2),
                )
            nc.vector.quantize_mx(out=x_codes[c][:].bitcast(FP8X4), scales=x_scales[c][:], in_=grouped[:])

        def pick(dst, m, lst, cols):
            nc.vector.tensor_copy(dst, page[m][:].indirect(lst[:, cols.start // 16 : cols.stop // 16]))

        for m in range(BLOCKS - 1):
            if m > 0:
                nc.vector.tensor_tensor(page[m][:].indirect(idx2[:]), h[m][:], gains[:], ALU.mult)
            ready = keep.tile([PARTS, P], F32, name=f"ready{m}", tag=f"shared_a{m + 1}", align_bytes=64)
            earlier = keep.tile([PARTS, P], F32, name=f"earlier{m}", tag=f"shared_b{m + 1}", align_bytes=64)
            pick(ready[:], m, idx3, slice(0, P))
            pick(earlier[:], m, idx4, slice(0, P))
            turn_x(m, [0, 1], ready[:, 0:HALF], "x_rows0")
            turn_x(m, [2], ready[:, HALF:P], "x_rows0")
            first_col = (m % 2) * 2 * P
            make_damp(m, slice(0, P), earlier[:], scratch[:, first_col : first_col + P], scratch[:, first_col + P : first_col + 2 * P])
            if m == BLOCKS - 2:
                warm = keep.tile([PARTS, 1], F32, name="warm")
                nc.scalar.activation(warm[:], scratch[:, first_col + P : first_col + P + 1], ACT.Tanh)
            if m == 0:
                w3_grouped = keep.tile([PARTS, H, PACK], BF16, name="w3_grouped", align_bytes=64)
                interleave(nc, w3_grouped[:], w3_raw[:])
                nc.vector.quantize_mx(
                    out=w3_codes[:].bitcast(FP8X4), scales=w3_scales[:], in_=w3_grouped[:].rearrange("p c t -> p (c t)")
                )

        def score(c, blocks, unit):
            n = widths[c]
            first = bank()
            second = bank()
            for i, m in enumerate(blocks):
                nc.tensor.matmul_mx(
                    out=first[:, i * n : (i + 1) * n],
                    lhsT=w4w[:, 2 * m * PARTS : 2 * (m + 1) * PARTS].bitcast(FP4X4),
                    lhsT_scale=w4s[:, m * PARTS : (m + 1) * PARTS],
                    rhs=x_codes[c][:].bitcast(FP8X4),
                    rhs_scale=x_scales[c][:],
                    start=True,
                    stop=True,
                )
            for i, m in enumerate(blocks):
                nc.tensor.matmul_mx(
                    out=second[:, i * n : (i + 1) * n],
                    lhsT=w3_codes[:, m * PARTS : (m + 1) * PARTS].bitcast(FP8X4),
                    lhsT_scale=w3_scales[:, m * PARTS : (m + 1) * PARTS],
                    rhs=x_codes[c][:].bitcast(FP8X4),
                    rhs_scale=x_scales[c][:],
                    start=True,
                    stop=True,
                )
            bounded = scratch[:, unit * HALF : (unit + 1) * HALF]
            nc.scalar.activation(bounded, first[:], ACT.Tanh)
            nc.vector.tensor_tensor(
                scores[:, blocks[0] : blocks[-1] + 1, chunks[c]],
                second[:].rearrange("p (b j) -> p b j", j=n),
                bounded.rearrange("p (b j) -> p b j", j=n),
                ALU.add,
            )

        def finish(m, half):
            cols = slice(half * HALF, (half + 1) * HALF)
            nc.vector.tensor_tensor(scores[:, m, cols], scores[:, m, cols], damp[:, m, cols], ALU.mult)
            nc.sync.dma_start(out=out[m * PARTS : (m + 1) * PARTS, cols], in_=scores[:, m, cols])

        m = BLOCKS - 1
        nc.vector.tensor_tensor(page[m][:].indirect(idx2[:]), h[m][:], gains[:], ALU.mult)
        ready = keep.tile([PARTS, P], F32, name="ready_last")
        for c in range(3):
            pick(ready[:, chunks[c]], m, idx3, chunks[c])
        pieces = [slice(0, 768), slice(768, 1024)]
        earlier_a = keep.tile([PARTS, 768], F32, name="earlier_a")
        pick(earlier_a[:], m, idx4, pieces[0])
        turn_x(m, [0], ready[:, chunks[0]], "x_rows0")
        turn_x(m, [1], ready[:, chunks[1]], "x_rows1")
        quantise_x(0)
        earlier_b = keep.tile([PARTS, 256], F32, name="earlier_b", tag="x_grouped0", align_bytes=64)
        pick(earlier_b[:], m, idx4, pieces[1])
        turn_x(m, [2], ready[:, chunks[2]], "x_rows1")
        quantise_x(1)
        quantise_x(2)
        score(0, [0, 1], 0)
        score(0, [2, 3], 1)
        score(1, [0, 1], 2)
        score(1, [2, 3], 3)
        for i in range(BLOCKS):
            if i < BLOCKS - 1:
                finish(i, 0)
            score(2, [i], BLOCKS + i)
        for i in range(BLOCKS - 1):
            finish(i, 1)
        mag = keep.tile([PARTS, P], F32, name="mag", tag="x_grouped1", align_bytes=64)
        for cols, piece in zip(pieces, (earlier_a, earlier_b)):
            nc.scalar.activation(mag[:, cols], piece[:], ACT.Abs, scale=ev_col[:, m : m + 1])
        for half in range(2):
            cols = slice(half * HALF, (half + 1) * HALF)
            root = scratch[:, (BLOCKS + half) * HALF : (BLOCKS + half + 1) * HALF]
            nc.scalar.activation(root, mag[:, cols], ACT.Abs_reciprocal_sqrt, bias=1.0)
            nc.scalar.activation(damp[:, m, cols], root, ACT.Square)
        for half in range(2):
            finish(m, half)
